import numpy as np
import ml_dtypes


def mxq(x, axis, fmt="e4m3"):
    dtype, down = {"e4m3": (ml_dtypes.float8_e4m3fn, 7), "e5m2": (ml_dtypes.float8_e5m2, 14)}[fmt]
    v = np.moveaxis(np.asarray(x, np.float32).astype(ml_dtypes.bfloat16).astype(np.float64), axis, -1)
    blocks = v.reshape(v.shape[:-1] + (-1, 32))
    amax = np.abs(blocks).max(-1, keepdims=True)
    byte = np.maximum(np.where(amax > 0, np.frexp(amax)[1] - 1 + 127, 0) - down, 1)
    scale = np.exp2(byte - 127.0)
    codes = (blocks / scale).astype(np.float32).astype(dtype).astype(np.float64)
    return np.moveaxis((codes * scale).reshape(v.shape), -1, axis)


WIDE = False


def mx_kscale(k):
    if not WIDE:
        return np.ones(k)
    levels = np.array([10, -10, 5, -5, 0])
    if k % 512:
        return np.exp2(np.random.permutation(np.resize(levels, k // 32))).repeat(32)
    a = np.empty((k // 512, 16))
    for p in range(k // 512):
        a[p, :8] = np.random.permutation(np.resize(levels, 8))
        for g in range(8):
            far = levels[np.abs(levels - a[p, g]) >= 10]
            a[p, g + 8] = far[np.random.randint(len(far))]
    return np.exp2(a.ravel()).repeat(32)


def f64(x):
    return np.asarray(x).astype(np.float64)


E2M1 = np.array([0.0, 0.5, 1.0, 1.5, 2.0, 3.0, 4.0, 6.0, -0.0, -0.5, -1.0, -1.5, -2.0, -3.0, -4.0, -6.0])


def pack_weight(w, fmt):
    k, n = w.shape
    w = f64(np.asarray(w, np.float32).astype(ml_dtypes.bfloat16)).reshape(k // 32, 32, n)
    amax = np.abs(w).max(1)
    if fmt == "e4m3":
        byte = np.frexp(amax)[1] - 1 + 127 - 7
    else:
        mant, ex = np.frexp(amax / 6.0)
        byte = np.where(mant > 0.5, ex, ex - 1) + 127
    byte = np.clip(np.where(amax > 0, byte, 1), 1, 254)
    scaled = (w * np.exp2(127.0 - byte)[:, None, :]).reshape(k, n).astype(np.float32)
    by_word = np.ascontiguousarray(scaled.reshape(k // 512, 128, 4, n).transpose(0, 1, 3, 2))
    if fmt == "e4m3":
        words = by_word.astype(ml_dtypes.float8_e4m3fn).view(np.uint8)
    else:
        c = by_word.astype(ml_dtypes.float4_e2m1fn).view(np.uint8) & 0xF
        words = (c[..., 0::2] | (c[..., 1::2] << 4)).reshape(k // 512, 128, 2 * n)
    return np.ascontiguousarray(words), np.ascontiguousarray(byte.astype(np.uint8).reshape(k // 512, 16, n))


def unpack_weight(words, scales, fmt):
    g, _, n = scales.shape
    words = np.ascontiguousarray(words).reshape(g, 128, n, -1)
    if fmt == "e4m3":
        vals = words.view(ml_dtypes.float8_e4m3fn).astype(np.float64)
    else:
        nib = np.empty((g, 128, n, 4), np.uint8)
        nib[..., 0::2] = words & 0xF
        nib[..., 1::2] = words >> 4
        vals = E2M1[nib]
    vals = vals * np.repeat(np.exp2(scales.astype(np.float64) - 127.0), 8, axis=1)[..., None]
    return vals.transpose(0, 1, 3, 2).reshape(g * 512, n)


K, L, T, B, N = 512, 1024, 1024, 512, 512


def setup_inputs():
    n = np.random.standard_normal
    fk = mx_kscale(K)
    fl = mx_kscale(L)
    wap = pack_weight(n((K, N)) * 1 / np.sqrt(K) * fk[:, None], "e2m1")
    wbp = pack_weight(n((K, N)) * 1 / np.sqrt(K) * fk[:, None], "e4m3")
    xqp = pack_weight(n((L, T)) / fl[:, None], "e2m1")
    wqp = pack_weight(n((L, N)) * 1 / np.sqrt(L) * fl[:, None], "e4m3")
    return {
        "xf": (n((K, T))).astype(np.float32),
        "fa": (np.random.uniform(0.5, 2.0, (K, 1)) / fk[:, None]).astype(np.float32),
        "fb": (np.random.uniform(0.5, 2.0, (K, 1)) / fk[:, None]).astype(np.float32),
        "wa_words": wap[0],
        "wa_scales": wap[1],
        "wb_words": wbp[0],
        "wb_scales": wbp[1],
        "xq_words": xqp[0],
        "xq_scales": xqp[1],
        "wq_words": wqp[0],
        "wq_scales": wqp[1],
    }


def reference(xf, fa, fb, wa_words, wa_scales, wb_words, wb_scales, xq_words, xq_scales, wq_words, wq_scales):
    wau = unpack_weight(wa_words, wa_scales, "e2m1")
    wbu = unpack_weight(wb_words, wb_scales, "e4m3")
    xqu = unpack_weight(xq_words, xq_scales, "e2m1")
    wqu = unpack_weight(wq_words, wq_scales, "e4m3")
    m = f64(xf).reshape(K, B, T // B).max(axis=2)
    u = m * f64(fa)
    mr = np.repeat(m, T // B, axis=1)
    d = (mr - f64(xf)) * f64(fb)
    uq = mxq(u, 0, "e4m3")
    za = wau.T @ uq
    ra = np.maximum(za, 0.0)
    zr = np.repeat(ra, T // B, axis=1)
    dq = mxq(d, 0, "e4m3")
    zb = wbu.T @ dq + wqu.T @ xqu
    y = zr + zb
    return y

@@ -1,0 +1,207 @@
+from contextlib import ExitStack
+
+import concourse.mybir as mybir
+
+K, L, T, B, N = 512, 1024, 1024, 512, 512
+FLOPS = 2 * N * (K * B + K * T + L * T)
+
+F32 = mybir.dt.float32
+BF16 = mybir.dt.bfloat16
+I32 = mybir.dt.int32
+U32 = mybir.dt.uint32
+U8 = mybir.dt.uint8
+FP8X4 = mybir.dt.float8_e4m3fn_x4
+FP4X4 = mybir.dt.float4_e2m1fn_x4
+ALU = mybir.AluOpType
+ACT = mybir.ActivationFunctionType
+
+P = 128
+PACK = 4
+CHUNK = 256
+PAIRS = CHUNK // 2
+CHUNKS = T // CHUNK
+HALF = 512
+TILES = N // P
+PASSES = L // (P * PACK)
+WALK = 4
+
+
+def tile_mix_group_peak_and_members_kernel(tc, xf, fa, fb, wa_words, wa_scales, wb_words, wb_scales,
+                                                xq_words, xq_scales, wq_words, wq_scales, out):
+    nc = tc.nc
+    with ExitStack() as ctx:
+        sb = ctx.enter_context(tc.tile_pool(name="sb", bufs=1))
+        ps = ctx.enter_context(tc.psum_pool(name="ps", bufs=1))
+        ctx.enter_context(tc.manual_schedule())
+
+        x = [sb.tile([P, PACK, CHUNK], F32, name="x%d" % c, align_bytes=64) for c in range(CHUNKS)]
+        fa_sb = sb.tile([P, PACK], F32, name="fa_sb")
+        fb_sb = sb.tile([P, PACK], F32, name="fb_sb")
+        fb_neg = sb.tile([P, PACK], F32, name="fb_neg")
+        wa_codes = sb.tile([P, 2 * N], U8, name="wa_codes", align_bytes=64)
+        wb_codes = sb.tile([P, N], U32, name="wb_codes", align_bytes=64)
+        wq_codes = sb.tile([P, PASSES, N], U32, name="wq_codes", align_bytes=64)
+        xq_codes = [sb.tile([P, PASSES, 2 * HALF], U8, name="xq_codes%d" % h, align_bytes=64) for h in range(2)]
+        wa_plane = sb.tile([P, 1, N], U8, name="wa_plane", align_bytes=64)
+        wb_plane = sb.tile([P, 1, N], U8, name="wb_plane", align_bytes=64)
+        wq_plane = sb.tile([P, PASSES, N], U8, name="wq_plane", align_bytes=64)
+        xq_plane = sb.tile([P, PASSES, T], U8, name="xq_plane", align_bytes=64)
+
+        for plane in (xq_plane, wq_plane, wa_plane, wb_plane):
+            nc.vector.memset(plane[:].bitcast(I32), 0)
+
+        def load_scales(queue, plane, scales, quadrants=range(4)):
+            for q in quadrants:
+                queue.dma_start(out=plane[32 * q : 32 * q + 4, :, :].bitcast(I32),
+                                in_=scales[:, 4 * q : 4 * q + 4, :].rearrange("z r n -> r z n").bitcast(I32))
+
+        x_rows = xf.rearrange("(p j) t -> p j t", j=PACK)
+
+        def load_x(c):
+            nc.sync.dma_start(out=x[c][:], in_=x_rows[:, :, c * CHUNK : (c + 1) * CHUNK])
+
+        def load_xq(h):
+            nc.sync.dma_start(out=xq_codes[h][:].bitcast(I32),
+                              in_=xq_words.rearrange("z p c -> p z c")[:, :, 2 * HALF * h : 2 * HALF * (h + 1)].bitcast(I32))
+
+        load_x(0)
+        nc.sync.dma_start(out=fb_sb[:], in_=fb.rearrange("(p j) o -> p (j o)", j=PACK))
+        nc.sync.dma_start(out=fa_sb[:], in_=fa.rearrange("(p j) o -> p (j o)", j=PACK))
+        load_x(1)
+        load_scales(nc.sync, wq_plane, wq_scales)
+        load_scales(nc.sync, xq_plane, xq_scales, range(2))
+        nc.sync.dma_start(out=wq_codes[:].bitcast(I32), in_=wq_words.rearrange("z p n r -> p z (n r)").bitcast(I32))
+        load_xq(0)
+        load_scales(nc.sync, xq_plane, xq_scales, range(2, 4))
+        load_x(2)
+        nc.sync.dma_start(out=wa_codes[:].bitcast(I32), in_=wa_words[0].bitcast(I32))
+        load_scales(nc.sync, wa_plane, wa_scales)
+        nc.sync.dma_start(out=wb_codes[:].bitcast(I32), in_=wb_words[0].rearrange("p n r -> p (n r)").bitcast(I32))
+        load_xq(1)
+        load_x(3)
+        load_scales(nc.sync, wb_plane, wb_scales)
+
+        nc.scalar.activation(out=fb_neg[:], in_=fb_sb[:], func=ACT.Copy, scale=-1.0)
+
+        u_in = [sb.tile([P, PAIRS, PACK], BF16, name="u_in%d" % c, align_bytes=64) for c in range(CHUNKS)]
+        d_in = [sb.tile([P, PAIRS, 2 * PACK], BF16, name="d_in%d" % c, align_bytes=64) for c in range(CHUNKS)]
+        u_codes = [sb.tile([P, PAIRS], U32, name="u_codes%d" % c, align_bytes=64) for c in range(CHUNKS)]
+        u_plane = [sb.tile([P, PAIRS], U8, name="u_plane%d" % c, align_bytes=64) for c in range(CHUNKS)]
+        d_codes = [sb.tile([P, CHUNK], U32, name="d_codes%d" % c, align_bytes=64) for c in range(CHUNKS)]
+        d_plane = [sb.tile([P, CHUNK], U8, name="d_plane%d" % c, align_bytes=64) for c in range(CHUNKS)]
+        ra = [sb.tile([P, TILES, CHUNK], F32, name="ra%d" % h, align_bytes=64) for h in range(2)]
+
+        def walk_rows(ap):
+            return ap.rearrange("p r (c i) -> p c r i", i=WALK)
+
+        def walk_columns(ap):
+            return ap.rearrange("p (c i) r -> p c r i", i=WALK)
+
+        def prepare(c):
+            even, odd = x[c][:, :, 0::2], x[c][:, :, 1::2]
+            gap = sb.tile([P, PACK, PAIRS], F32, name="gap%d" % c, align_bytes=64)
+            d_rows = sb.tile([P, 2 * PACK, PAIRS], BF16, name="d_rows%d" % c, align_bytes=64)
+            nc.vector.tensor_tensor(out=gap[:], in0=odd, in1=even, op=ALU.subtract)
+            last = c == CHUNKS - 1
+            if last:
+                peak = sb.tile([P, PAIRS, PACK], F32, name="peak%d" % c, align_bytes=64)
+                nc.vector.tensor_tensor(out=walk_columns(peak[:]), in0=walk_rows(even), in1=walk_rows(odd), op=ALU.max)
+            else:
+                peak = sb.tile([P, PACK, PAIRS], F32, name="peak%d" % c, align_bytes=64)
+                nc.vector.tensor_tensor(out=peak[:], in0=even, in1=odd, op=ALU.max)
+            for j in range(PACK):
+                nc.vector.tensor_scalar(out=d_rows[:, j, :], in0=gap[:, j, :], scalar1=0.0, scalar2=fb_sb[:, j : j + 1],
+                                        op0=ALU.max, op1=ALU.mult)
+            for j in range(PACK):
+                nc.vector.tensor_scalar(out=d_rows[:, PACK + j, :], in0=gap[:, j, :], scalar1=0.0, scalar2=fb_neg[:, j : j + 1],
+                                        op0=ALU.min, op1=ALU.mult)
+            if last:
+                nc.vector.tensor_tensor(out=u_in[c][:], in0=peak[:], in1=fa_sb[:].unsqueeze(1).to_broadcast([P, PAIRS, PACK]),
+                                        op=ALU.mult)
+                nc.scalar.copy(out=walk_columns(d_in[c][:]), in_=walk_rows(d_rows[:]))
+            else:
+                u_rows = sb.tile([P, PACK, PAIRS], BF16, name="u_rows%d" % c, align_bytes=64)
+                for j in range(PACK):
+                    nc.scalar.activation(out=u_rows[:, j, :], in_=peak[:, j, :], func=ACT.Copy, scale=fa_sb[:, j : j + 1])
+                nc.scalar.copy(out=walk_columns(d_in[c][:]), in_=walk_rows(d_rows[:]))
+                nc.scalar.copy(out=walk_columns(u_in[c][:]), in_=walk_rows(u_rows[:]))
+
+        def quantize_d(c):
+            nc.vector.quantize_mx(out=d_codes[c][:].bitcast(FP8X4), scales=d_plane[c][:], in_=d_in[c][:].rearrange("p b r -> p (b r)"))
+
+        def quantize_u(c):
+            nc.vector.quantize_mx(out=u_codes[c][:].bitcast(FP8X4), scales=u_plane[c][:], in_=u_in[c][:].rearrange("p b j -> p (b j)"))
+
+        za = {}
+        zb = {}
+
+        def peak_product(c):
+            za[c] = ps.tile([P, TILES, PAIRS], F32, name="za%d" % c, tag="za%d" % (c % 2))
+            for i in range(TILES):
+                nc.tensor.matmul_mx(out=za[c][:, i, :], lhsT=wa_codes[:, 2 * P * i : 2 * P * (i + 1)].bitcast(FP4X4),
+                                    lhsT_scale=wa_plane[:, 0, P * i : P * (i + 1)], rhs=u_codes[c][:].bitcast(FP8X4),
+                                    rhs_scale=u_plane[c][:], start=True, stop=True)
+
+        def relu(c):
+            nc.scalar.activation(out=ra[c // 2][:, :, (c % 2) * PAIRS : (c % 2 + 1) * PAIRS], in_=za[c][:], func=ACT.Relu)
+
+        def second_product(h, i, bank):
+            zb[h, i] = ps.tile([P, HALF], F32, name="zb%d_%d" % (h, i), tag="zb%d" % bank)
+            for z in range(PASSES):
+                nc.tensor.matmul_mx(out=zb[h, i][:], lhsT=wq_codes[:, z, P * i : P * (i + 1)].bitcast(FP8X4),
+                                    lhsT_scale=wq_plane[:, z, P * i : P * (i + 1)], rhs=xq_codes[h][:, z, :].bitcast(FP4X4),
+                                    rhs_scale=xq_plane[:, z, HALF * h : HALF * (h + 1)], start=(z == 0), stop=False)
+
+        def distance_product(c, i):
+            nc.tensor.matmul_mx(out=zb[c // 2, i][:, (c % 2) * CHUNK : (c % 2 + 1) * CHUNK],
+                                lhsT=wb_codes[:, P * i : P * (i + 1)].bitcast(FP8X4), lhsT_scale=wb_plane[:, 0, P * i : P * (i + 1)],
+                                rhs=d_codes[c][:].bitcast(FP8X4), rhs_scale=d_plane[c][:], start=False, stop=(c % 2 == 1))
+
+        def finish(h, i):
+            res = sb.tile([P, CHUNK, 2], F32, name="res%d_%d" % (h, i), align_bytes=64)
+            nc.vector.tensor_tensor(out=res[:], in0=zb[h, i][:].rearrange("p (b e) -> p b e", e=2),
+                                    in1=ra[h][:, i, :].unsqueeze(2).to_broadcast([P, CHUNK, 2]), op=ALU.add)
+            nc.sync.dma_start(out=out[P * i : P * (i + 1), HALF * h : HALF * (h + 1)], in_=res[:].rearrange("p b e -> p (b e)"))
+
+        prepare(0)
+        prepare(1)
+        for i in range(TILES):
+            second_product(0, i, i)
+        quantize_d(0)
+        quantize_u(0)
+        peak_product(0)
+        for i in range(TILES):
+            distance_product(0, i)
+        second_product(1, 0, 4)
+        second_product(1, 1, 5)
+        relu(0)
+        prepare(2)
+        quantize_d(1)
+        quantize_u(1)
+        peak_product(1)
+        for i in range(TILES):
+            distance_product(1, i)
+        relu(1)
+        prepare(3)
+        quantize_d(2)
+        quantize_u(2)
+        quantize_u(3)
+        peak_product(2)
+        peak_product(3)
+        relu(2)
+        relu(3)
+        distance_product(2, 0)
+        distance_product(2, 1)
+        finish(0, 0)
+        second_product(1, 2, 0)
+        distance_product(2, 2)
+        finish(0, 1)
+        second_product(1, 3, 1)
+        distance_product(2, 3)
+        quantize_d(3)
+        for i in range(TILES):
+            distance_product(3, i)
+        finish(0, 2)
+        finish(0, 3)
+        for i in range(TILES):
+            finish(1, i)

@@ -20,10 +20,9 @@ PACK = 4
 CHUNK = 256
 PAIRS = CHUNK // 2
 CHUNKS = T // CHUNK
-HALF = 512
+HALF = 2 * CHUNK
 TILES = N // P
 PASSES = L // (P * PACK)
-WALK = 4
 
 
 def tile_mix_group_peak_and_members_kernel(tc, xf, fa, fb, wa_words, wa_scales, wb_words, wb_scales,
@@ -40,167 +39,188 @@ def tile_mix_group_peak_and_members_kernel(tc, xf, fa, fb, wa_words, wa_scales, 
         fb_neg = sb.tile([P, PACK], F32, name="fb_neg")
         wa_codes = sb.tile([P, 2 * N], U8, name="wa_codes", align_bytes=64)
         wb_codes = sb.tile([P, N], U32, name="wb_codes", align_bytes=64)
-        wq_codes = sb.tile([P, PASSES, N], U32, name="wq_codes", align_bytes=64)
+        wq_codes = [sb.tile([P, PASSES, 2 * P], U32, name="wq_codes%d" % g, align_bytes=64) for g in range(2)]
         xq_codes = [sb.tile([P, PASSES, 2 * HALF], U8, name="xq_codes%d" % h, align_bytes=64) for h in range(2)]
         wa_plane = sb.tile([P, 1, N], U8, name="wa_plane", align_bytes=64)
         wb_plane = sb.tile([P, 1, N], U8, name="wb_plane", align_bytes=64)
         wq_plane = sb.tile([P, PASSES, N], U8, name="wq_plane", align_bytes=64)
         xq_plane = sb.tile([P, PASSES, T], U8, name="xq_plane", align_bytes=64)
 
-        for plane in (xq_plane, wq_plane, wa_plane, wb_plane):
+        for plane in (wb_plane, wa_plane, wq_plane, xq_plane):
             nc.vector.memset(plane[:].bitcast(I32), 0)
-
-        def load_scales(queue, plane, scales, quadrants=range(4)):
-            for q in quadrants:
-                queue.dma_start(out=plane[32 * q : 32 * q + 4, :, :].bitcast(I32),
-                                in_=scales[:, 4 * q : 4 * q + 4, :].rearrange("z r n -> r z n").bitcast(I32))
 
         x_rows = xf.rearrange("(p j) t -> p j t", j=PACK)
 
-        def load_x(c):
-            nc.sync.dma_start(out=x[c][:], in_=x_rows[:, :, c * CHUNK : (c + 1) * CHUNK])
+        def load_x(c, rows=slice(0, PACK)):
+            nc.sync.dma_start(out=x[c][:, rows, :], in_=x_rows[:, rows, c * CHUNK : (c + 1) * CHUNK])
 
-        def load_xq(h):
-            nc.sync.dma_start(out=xq_codes[h][:].bitcast(I32),
-                              in_=xq_words.rearrange("z p c -> p z c")[:, :, 2 * HALF * h : 2 * HALF * (h + 1)].bitcast(I32))
+        def load_factor(tile, factor):
+            nc.sync.dma_start(out=tile[:], in_=factor.rearrange("(p j) o -> p (j o)", j=PACK))
 
-        load_x(0)
-        nc.sync.dma_start(out=fb_sb[:], in_=fb.rearrange("(p j) o -> p (j o)", j=PACK))
-        nc.sync.dma_start(out=fa_sb[:], in_=fa.rearrange("(p j) o -> p (j o)", j=PACK))
+        def load_bytes(tile, words):
+            nc.sync.dma_start(out=tile[:].bitcast(I32), in_=words.bitcast(I32))
+
+        def load_scales(plane, scales, rows):
+            for r in rows:
+                nc.sync.dma_start(out=plane[r:P:32, :, :].bitcast(I32),
+                                  in_=scales[:, r:16:4, :].rearrange("z q n -> q z n").bitcast(I32))
+
+        wq_bytes = wq_words.rearrange("z p n r -> p z (n r)")
+        xq_bytes = xq_words.rearrange("z p c -> p z c")
+        load_x(0, slice(0, 2))
+        load_factor(fb_sb, fb)
+        load_x(0, slice(2, 4))
+        load_factor(fa_sb, fa)
         load_x(1)
-        load_scales(nc.sync, wq_plane, wq_scales)
-        load_scales(nc.sync, xq_plane, xq_scales, range(2))
-        nc.sync.dma_start(out=wq_codes[:].bitcast(I32), in_=wq_words.rearrange("z p n r -> p z (n r)").bitcast(I32))
-        load_xq(0)
-        load_scales(nc.sync, xq_plane, xq_scales, range(2, 4))
+        load_scales(wb_plane, wb_scales, (0, 1, 2))
         load_x(2)
-        nc.sync.dma_start(out=wa_codes[:].bitcast(I32), in_=wa_words[0].bitcast(I32))
-        load_scales(nc.sync, wa_plane, wa_scales)
-        nc.sync.dma_start(out=wb_codes[:].bitcast(I32), in_=wb_words[0].rearrange("p n r -> p (n r)").bitcast(I32))
-        load_xq(1)
+        load_scales(wb_plane, wb_scales, (3,))
+        load_scales(wa_plane, wa_scales, (0,))
+        load_bytes(wb_codes, wb_words[0].rearrange("p n r -> p (n r)"))
+        load_scales(wa_plane, wa_scales, (1, 2, 3))
         load_x(3)
-        load_scales(nc.sync, wb_plane, wb_scales)
+        load_scales(wq_plane, wq_scales, (0, 1))
+        load_bytes(wa_codes, wa_words[0])
+        load_scales(wq_plane, wq_scales, (2, 3))
+        load_scales(xq_plane, xq_scales, (0,))
+        load_bytes(wq_codes[0], wq_bytes[:, :, : 8 * P])
+        load_scales(xq_plane, xq_scales, (1, 2, 3))
+        load_bytes(xq_codes[0], xq_bytes[:, :, : 2 * HALF])
+        load_bytes(wq_codes[1], wq_bytes[:, :, 8 * P :])
+        load_bytes(xq_codes[1], xq_bytes[:, :, 2 * HALF :])
 
         nc.scalar.activation(out=fb_neg[:], in_=fb_sb[:], func=ACT.Copy, scale=-1.0)
 
         u_in = [sb.tile([P, PAIRS, PACK], BF16, name="u_in%d" % c, align_bytes=64) for c in range(CHUNKS)]
         d_in = [sb.tile([P, PAIRS, 2 * PACK], BF16, name="d_in%d" % c, align_bytes=64) for c in range(CHUNKS)]
-        u_codes = [sb.tile([P, PAIRS], U32, name="u_codes%d" % c, align_bytes=64) for c in range(CHUNKS)]
-        u_plane = [sb.tile([P, PAIRS], U8, name="u_plane%d" % c, align_bytes=64) for c in range(CHUNKS)]
+        d_rows = [sb.tile([P, 2 * PACK, PAIRS], BF16, name="d_rows%d" % c, align_bytes=64) for c in range(CHUNKS)]
+        u_codes = [sb.tile([P, 2 * PAIRS], U32, name="u_codes%d" % h, align_bytes=64) for h in range(2)]
+        u_plane = [sb.tile([P, 2 * PAIRS], U8, name="u_plane%d" % h, align_bytes=64) for h in range(2)]
         d_codes = [sb.tile([P, CHUNK], U32, name="d_codes%d" % c, align_bytes=64) for c in range(CHUNKS)]
         d_plane = [sb.tile([P, CHUNK], U8, name="d_plane%d" % c, align_bytes=64) for c in range(CHUNKS)]
-        ra = [sb.tile([P, TILES, CHUNK], F32, name="ra%d" % h, align_bytes=64) for h in range(2)]
 
-        def walk_rows(ap):
-            return ap.rearrange("p r (c i) -> p c r i", i=WALK)
+        def by_rows(ap, run):
+            return ap.rearrange("p r (c i) -> p c r i", i=run)
 
-        def walk_columns(ap):
-            return ap.rearrange("p (c i) r -> p c r i", i=WALK)
+        def by_columns(ap, run):
+            return ap.rearrange("p (c i) r -> p c r i", i=run)
 
-        def prepare(c):
+        def interleave_d(c):
+            nc.scalar.copy(out=by_columns(d_in[c][:], 2), in_=by_rows(d_rows[c][:], 2))
+
+        def prepare(c, row_groups=(slice(0, PACK),)):
             even, odd = x[c][:, :, 0::2], x[c][:, :, 1::2]
+            peak = sb.tile([P, PACK, PAIRS], F32, name="peak%d" % c, align_bytes=64)
             gap = sb.tile([P, PACK, PAIRS], F32, name="gap%d" % c, align_bytes=64)
-            d_rows = sb.tile([P, 2 * PACK, PAIRS], BF16, name="d_rows%d" % c, align_bytes=64)
-            nc.vector.tensor_tensor(out=gap[:], in0=odd, in1=even, op=ALU.subtract)
-            last = c == CHUNKS - 1
-            if last:
-                peak = sb.tile([P, PAIRS, PACK], F32, name="peak%d" % c, align_bytes=64)
-                nc.vector.tensor_tensor(out=walk_columns(peak[:]), in0=walk_rows(even), in1=walk_rows(odd), op=ALU.max)
-            else:
-                peak = sb.tile([P, PACK, PAIRS], F32, name="peak%d" % c, align_bytes=64)
-                nc.vector.tensor_tensor(out=peak[:], in0=even, in1=odd, op=ALU.max)
+            u_rows = sb.tile([P, PACK, PAIRS], BF16, name="u_rows%d" % c, align_bytes=64)
+            for rows in row_groups:
+                nc.vector.tensor_tensor(out=gap[:, rows, :], in0=odd[:, rows, :], in1=even[:, rows, :], op=ALU.subtract)
+                nc.vector.tensor_tensor(out=peak[:, rows, :], in0=even[:, rows, :], in1=odd[:, rows, :], op=ALU.max)
+            distances(c, gap)
             for j in range(PACK):
-                nc.vector.tensor_scalar(out=d_rows[:, j, :], in0=gap[:, j, :], scalar1=0.0, scalar2=fb_sb[:, j : j + 1],
-                                        op0=ALU.max, op1=ALU.mult)
-            for j in range(PACK):
-                nc.vector.tensor_scalar(out=d_rows[:, PACK + j, :], in0=gap[:, j, :], scalar1=0.0, scalar2=fb_neg[:, j : j + 1],
-                                        op0=ALU.min, op1=ALU.mult)
-            if last:
-                nc.vector.tensor_tensor(out=u_in[c][:], in0=peak[:], in1=fa_sb[:].unsqueeze(1).to_broadcast([P, PAIRS, PACK]),
-                                        op=ALU.mult)
-                nc.scalar.copy(out=walk_columns(d_in[c][:]), in_=walk_rows(d_rows[:]))
-            else:
-                u_rows = sb.tile([P, PACK, PAIRS], BF16, name="u_rows%d" % c, align_bytes=64)
+                nc.scalar.activation(out=u_rows[:, j, :], in_=peak[:, j, :], func=ACT.Copy, scale=fa_sb[:, j : j + 1])
+            interleave_d(c)
+            nc.scalar.copy(out=by_columns(u_in[c][:], 4), in_=by_rows(u_rows[:], 4))
+
+        def distances(c, gap):
+            for e, (clamp, factor) in enumerate(((ALU.max, fb_sb), (ALU.min, fb_neg))):
                 for j in range(PACK):
-                    nc.scalar.activation(out=u_rows[:, j, :], in_=peak[:, j, :], func=ACT.Copy, scale=fa_sb[:, j : j + 1])
-                nc.scalar.copy(out=walk_columns(d_in[c][:]), in_=walk_rows(d_rows[:]))
-                nc.scalar.copy(out=walk_columns(u_in[c][:]), in_=walk_rows(u_rows[:]))
+                    nc.vector.tensor_scalar(out=d_rows[c][:, PACK * e + j, :], in0=gap[:, j, :], scalar1=0.0,
+                                            scalar2=factor[:, j : j + 1], op0=clamp, op1=ALU.mult)
+
+        def prepare_last(c):
+            even, odd = x[c][:, :, 0::2], x[c][:, :, 1::2]
+            peak = sb.tile([P, PAIRS, PACK], F32, name="peak%d" % c, align_bytes=64)
+            gap = sb.tile([P, PACK, PAIRS], F32, name="gap%d" % c, align_bytes=64)
+            nc.vector.tensor_tensor(out=gap[:], in0=odd, in1=even, op=ALU.subtract)
+            nc.vector.tensor_tensor(out=by_columns(peak[:], 2), in0=by_rows(even, 2), in1=by_rows(odd, 2), op=ALU.max)
+            distances(c, gap)
+            nc.vector.tensor_tensor(out=u_in[c][:], in0=peak[:], in1=fa_sb[:].unsqueeze(1).to_broadcast([P, PAIRS, PACK]),
+                                    op=ALU.mult)
 
         def quantize_d(c):
-            nc.vector.quantize_mx(out=d_codes[c][:].bitcast(FP8X4), scales=d_plane[c][:], in_=d_in[c][:].rearrange("p b r -> p (b r)"))
+            nc.vector.quantize_mx(out=d_codes[c][:].bitcast(FP8X4), scales=d_plane[c][:],
+                                  in_=d_in[c][:].rearrange("p b r -> p (b r)"))
 
         def quantize_u(c):
-            nc.vector.quantize_mx(out=u_codes[c][:].bitcast(FP8X4), scales=u_plane[c][:], in_=u_in[c][:].rearrange("p b j -> p (b j)"))
+            cols = slice((c % 2) * PAIRS, (c % 2 + 1) * PAIRS)
+            nc.vector.quantize_mx(out=u_codes[c // 2][:, cols].bitcast(FP8X4), scales=u_plane[c // 2][:, cols],
+                                  in_=u_in[c][:].rearrange("p b j -> p (b j)"))
 
-        za = {}
-        zb = {}
+        za, ra, zb = {}, {}, {}
 
-        def peak_product(c):
-            za[c] = ps.tile([P, TILES, PAIRS], F32, name="za%d" % c, tag="za%d" % (c % 2))
-            for i in range(TILES):
-                nc.tensor.matmul_mx(out=za[c][:, i, :], lhsT=wa_codes[:, 2 * P * i : 2 * P * (i + 1)].bitcast(FP4X4),
-                                    lhsT_scale=wa_plane[:, 0, P * i : P * (i + 1)], rhs=u_codes[c][:].bitcast(FP8X4),
-                                    rhs_scale=u_plane[c][:], start=True, stop=True)
+        def peak_product(h):
+            for g in range(2):
+                za[h, g] = ps.tile([P, 2, 2 * PAIRS], F32, name="za%d_%d" % (h, g), tag="za%d" % g)
+                for i in (2 * g, 2 * g + 1):
+                    nc.tensor.matmul_mx(out=za[h, g][:, i % 2, :], lhsT=wa_codes[:, 2 * P * i : 2 * P * (i + 1)].bitcast(FP4X4),
+                                        lhsT_scale=wa_plane[:, 0, P * i : P * (i + 1)], rhs=u_codes[h][:].bitcast(FP8X4),
+                                        rhs_scale=u_plane[h][:], start=True, stop=True)
 
-        def relu(c):
-            nc.scalar.activation(out=ra[c // 2][:, :, (c % 2) * PAIRS : (c % 2 + 1) * PAIRS], in_=za[c][:], func=ACT.Relu)
+        def relu(h, g):
+            ra[h, g] = sb.tile([P, 2, 2 * PAIRS], F32, name="ra%d_%d" % (h, g), align_bytes=64)
+            nc.scalar.activation(out=ra[h, g][:], in_=za[h, g][:], func=ACT.Relu)
 
-        def second_product(h, i, bank):
+        def open_bank(h, i, bank):
             zb[h, i] = ps.tile([P, HALF], F32, name="zb%d_%d" % (h, i), tag="zb%d" % bank)
-            for z in range(PASSES):
-                nc.tensor.matmul_mx(out=zb[h, i][:], lhsT=wq_codes[:, z, P * i : P * (i + 1)].bitcast(FP8X4),
-                                    lhsT_scale=wq_plane[:, z, P * i : P * (i + 1)], rhs=xq_codes[h][:, z, :].bitcast(FP4X4),
-                                    rhs_scale=xq_plane[:, z, HALF * h : HALF * (h + 1)], start=(z == 0), stop=False)
 
-        def distance_product(c, i):
+        def second_product(h, i, start=False, stop=False):
+            for z in range(PASSES):
+                nc.tensor.matmul_mx(out=zb[h, i][:], lhsT=wq_codes[i // 2][:, z, P * (i % 2) : P * (i % 2 + 1)].bitcast(FP8X4),
+                                    lhsT_scale=wq_plane[:, z, P * i : P * (i + 1)], rhs=xq_codes[h][:, z, :].bitcast(FP4X4),
+                                    rhs_scale=xq_plane[:, z, HALF * h : HALF * (h + 1)],
+                                    start=start and z == 0, stop=stop and z == PASSES - 1)
+
+        def distance_product(c, i, start=False, stop=False):
             nc.tensor.matmul_mx(out=zb[c // 2, i][:, (c % 2) * CHUNK : (c % 2 + 1) * CHUNK],
                                 lhsT=wb_codes[:, P * i : P * (i + 1)].bitcast(FP8X4), lhsT_scale=wb_plane[:, 0, P * i : P * (i + 1)],
-                                rhs=d_codes[c][:].bitcast(FP8X4), rhs_scale=d_plane[c][:], start=False, stop=(c % 2 == 1))
+                                rhs=d_codes[c][:].bitcast(FP8X4), rhs_scale=d_plane[c][:], start=start, stop=stop)
 
         def finish(h, i):
-            res = sb.tile([P, CHUNK, 2], F32, name="res%d_%d" % (h, i), align_bytes=64)
+            res = sb.tile([P, 2 * PAIRS, 2], F32, name="res%d_%d" % (h, i), align_bytes=64)
             nc.vector.tensor_tensor(out=res[:], in0=zb[h, i][:].rearrange("p (b e) -> p b e", e=2),
-                                    in1=ra[h][:, i, :].unsqueeze(2).to_broadcast([P, CHUNK, 2]), op=ALU.add)
+                                    in1=ra[h, i // 2][:, i % 2, :].unsqueeze(2).to_broadcast([P, 2 * PAIRS, 2]), op=ALU.add)
             nc.sync.dma_start(out=out[P * i : P * (i + 1), HALF * h : HALF * (h + 1)], in_=res[:].rearrange("p b e -> p (b e)"))
 
-        prepare(0)
+        prepare(0, (slice(0, 2), slice(2, 4)))
         prepare(1)
-        for i in range(TILES):
-            second_product(0, i, i)
         quantize_d(0)
         quantize_u(0)
-        peak_product(0)
         for i in range(TILES):
-            distance_product(0, i)
-        second_product(1, 0, 4)
-        second_product(1, 1, 5)
-        relu(0)
+            open_bank(0, i, i)
+            distance_product(0, i, start=True)
         prepare(2)
         quantize_d(1)
         quantize_u(1)
-        peak_product(1)
+        peak_product(0)
         for i in range(TILES):
             distance_product(1, i)
-        relu(1)
-        prepare(3)
-        quantize_d(2)
-        quantize_u(2)
-        quantize_u(3)
-        peak_product(2)
-        peak_product(3)
-        relu(2)
-        relu(3)
-        distance_product(2, 0)
-        distance_product(2, 1)
-        finish(0, 0)
-        second_product(1, 2, 0)
-        distance_product(2, 2)
-        finish(0, 1)
-        second_product(1, 3, 1)
-        distance_product(2, 3)
-        quantize_d(3)
         for i in range(TILES):
-            distance_product(3, i)
+            second_product(0, i, stop=True)
+        prepare_last(3)
+        relu(0, 0)
+        interleave_d(3)
+        relu(0, 1)
+        quantize_u(2)
+        quantize_d(2)
+        quantize_u(3)
+        peak_product(1)
+        relu(1, 0)
+        relu(1, 1)
+        for i in range(2):
+            open_bank(1, i, TILES + i)
+            second_product(1, i, start=True)
+            distance_product(2, i)
+        finish(0, 0)
+        quantize_d(3)
+        finish(0, 1)
+        for i in range(2):
+            distance_product(3, i, stop=True)
+        for i in range(2, TILES):
+            open_bank(1, i, i - 2)
+            second_product(1, i, start=True)
+            distance_product(2, i)
+            distance_product(3, i, stop=True)
         finish(0, 2)
         finish(0, 3)
         for i in range(TILES):

from contextlib import ExitStack

import concourse.mybir as mybir

K, L, T, B, N = 512, 1024, 1024, 512, 512
FLOPS = 2 * N * (K * B + K * T + L * T)

F32 = mybir.dt.float32
BF16 = mybir.dt.bfloat16
I32 = mybir.dt.int32
U32 = mybir.dt.uint32
U8 = mybir.dt.uint8
FP8X4 = mybir.dt.float8_e4m3fn_x4
FP4X4 = mybir.dt.float4_e2m1fn_x4
ALU = mybir.AluOpType
ACT = mybir.ActivationFunctionType

P = 128
PACK = 4
CHUNK = 256
PAIRS = CHUNK // 2
CHUNKS = T // CHUNK
HALF = 2 * CHUNK
TILES = N // P
PASSES = L // (P * PACK)


def tile_mix_group_peak_and_members_kernel(tc, xf, fa, fb, wa_words, wa_scales, wb_words, wb_scales,
                                                xq_words, xq_scales, wq_words, wq_scales, out):
    nc = tc.nc
    with ExitStack() as ctx:
        sb = ctx.enter_context(tc.tile_pool(name="sb", bufs=1))
        ps = ctx.enter_context(tc.psum_pool(name="ps", bufs=1))
        ctx.enter_context(tc.manual_schedule())

        x = [sb.tile([P, PACK, CHUNK], F32, name="x%d" % c, align_bytes=64) for c in range(CHUNKS)]
        fa_sb = sb.tile([P, PACK], F32, name="fa_sb")
        fb_sb = sb.tile([P, PACK], F32, name="fb_sb")
        fb_neg = sb.tile([P, PACK], F32, name="fb_neg")
        wa_codes = sb.tile([P, 2 * N], U8, name="wa_codes", align_bytes=64)
        wb_codes = sb.tile([P, N], U32, name="wb_codes", align_bytes=64)
        wq_codes = [sb.tile([P, PASSES, 2 * P], U32, name="wq_codes%d" % g, align_bytes=64) for g in range(2)]
        xq_codes = [sb.tile([P, PASSES, 2 * HALF], U8, name="xq_codes%d" % h, align_bytes=64) for h in range(2)]
        wa_plane = sb.tile([P, 1, N], U8, name="wa_plane", align_bytes=64)
        wb_plane = sb.tile([P, 1, N], U8, name="wb_plane", align_bytes=64)
        wq_plane = sb.tile([P, PASSES, N], U8, name="wq_plane", align_bytes=64)
        xq_plane = sb.tile([P, PASSES, T], U8, name="xq_plane", align_bytes=64)

        for plane in (wb_plane, wa_plane, wq_plane, xq_plane):
            nc.vector.memset(plane[:].bitcast(I32), 0)

        x_rows = xf.rearrange("(p j) t -> p j t", j=PACK)

        def load_x(c, rows=slice(0, PACK)):
            nc.sync.dma_start(out=x[c][:, rows, :], in_=x_rows[:, rows, c * CHUNK : (c + 1) * CHUNK])

        def load_factor(tile, factor):
            nc.sync.dma_start(out=tile[:], in_=factor.rearrange("(p j) o -> p (j o)", j=PACK))

        def load_bytes(tile, words):
            nc.sync.dma_start(out=tile[:].bitcast(I32), in_=words.bitcast(I32))

        def load_scales(plane, scales, rows):
            for r in rows:
                nc.sync.dma_start(out=plane[r:P:32, :, :].bitcast(I32),
                                  in_=scales[:, r:16:4, :].rearrange("z q n -> q z n").bitcast(I32))

        wq_bytes = wq_words.rearrange("z p n r -> p z (n r)")
        xq_bytes = xq_words.rearrange("z p c -> p z c")
        load_x(0, slice(0, 2))
        load_factor(fb_sb, fb)
        load_x(0, slice(2, 4))
        load_factor(fa_sb, fa)
        load_x(1)
        load_scales(wb_plane, wb_scales, (0, 1, 2))
        load_x(2)
        load_scales(wb_plane, wb_scales, (3,))
        load_scales(wa_plane, wa_scales, (0,))
        load_bytes(wb_codes, wb_words[0].rearrange("p n r -> p (n r)"))
        load_scales(wa_plane, wa_scales, (1, 2, 3))
        load_x(3)
        load_scales(wq_plane, wq_scales, (0, 1))
        load_bytes(wa_codes, wa_words[0])
        load_scales(wq_plane, wq_scales, (2, 3))
        load_scales(xq_plane, xq_scales, (0,))
        load_bytes(wq_codes[0], wq_bytes[:, :, : 8 * P])
        load_scales(xq_plane, xq_scales, (1, 2, 3))
        load_bytes(xq_codes[0], xq_bytes[:, :, : 2 * HALF])
        load_bytes(wq_codes[1], wq_bytes[:, :, 8 * P :])
        load_bytes(xq_codes[1], xq_bytes[:, :, 2 * HALF :])

        nc.scalar.activation(out=fb_neg[:], in_=fb_sb[:], func=ACT.Copy, scale=-1.0)

        u_in = [sb.tile([P, PAIRS, PACK], BF16, name="u_in%d" % c, align_bytes=64) for c in range(CHUNKS)]
        d_in = [sb.tile([P, PAIRS, 2 * PACK], BF16, name="d_in%d" % c, align_bytes=64) for c in range(CHUNKS)]
        d_rows = [sb.tile([P, 2 * PACK, PAIRS], BF16, name="d_rows%d" % c, align_bytes=64) for c in range(CHUNKS)]
        u_codes = [sb.tile([P, 2 * PAIRS], U32, name="u_codes%d" % h, align_bytes=64) for h in range(2)]
        u_plane = [sb.tile([P, 2 * PAIRS], U8, name="u_plane%d" % h, align_bytes=64) for h in range(2)]
        d_codes = [sb.tile([P, CHUNK], U32, name="d_codes%d" % c, align_bytes=64) for c in range(CHUNKS)]
        d_plane = [sb.tile([P, CHUNK], U8, name="d_plane%d" % c, align_bytes=64) for c in range(CHUNKS)]

        def by_rows(ap, run):
            return ap.rearrange("p r (c i) -> p c r i", i=run)

        def by_columns(ap, run):
            return ap.rearrange("p (c i) r -> p c r i", i=run)

        def interleave_d(c):
            nc.scalar.copy(out=by_columns(d_in[c][:], 2), in_=by_rows(d_rows[c][:], 2))

        def prepare(c, row_groups=(slice(0, PACK),)):
            even, odd = x[c][:, :, 0::2], x[c][:, :, 1::2]
            peak = sb.tile([P, PACK, PAIRS], F32, name="peak%d" % c, align_bytes=64)
            gap = sb.tile([P, PACK, PAIRS], F32, name="gap%d" % c, align_bytes=64)
            u_rows = sb.tile([P, PACK, PAIRS], BF16, name="u_rows%d" % c, align_bytes=64)
            for rows in row_groups:
                nc.vector.tensor_tensor(out=gap[:, rows, :], in0=odd[:, rows, :], in1=even[:, rows, :], op=ALU.subtract)
                nc.vector.tensor_tensor(out=peak[:, rows, :], in0=even[:, rows, :], in1=odd[:, rows, :], op=ALU.max)
            distances(c, gap)
            for j in range(PACK):
                nc.scalar.activation(out=u_rows[:, j, :], in_=peak[:, j, :], func=ACT.Copy, scale=fa_sb[:, j : j + 1])
            interleave_d(c)
            nc.scalar.copy(out=by_columns(u_in[c][:], 4), in_=by_rows(u_rows[:], 4))

        def distances(c, gap):
            for e, (clamp, factor) in enumerate(((ALU.max, fb_sb), (ALU.min, fb_neg))):
                for j in range(PACK):
                    nc.vector.tensor_scalar(out=d_rows[c][:, PACK * e + j, :], in0=gap[:, j, :], scalar1=0.0,
                                            scalar2=factor[:, j : j + 1], op0=clamp, op1=ALU.mult)

        def prepare_last(c):
            even, odd = x[c][:, :, 0::2], x[c][:, :, 1::2]
            peak = sb.tile([P, PAIRS, PACK], F32, name="peak%d" % c, align_bytes=64)
            gap = sb.tile([P, PACK, PAIRS], F32, name="gap%d" % c, align_bytes=64)
            nc.vector.tensor_tensor(out=gap[:], in0=odd, in1=even, op=ALU.subtract)
            nc.vector.tensor_tensor(out=by_columns(peak[:], 2), in0=by_rows(even, 2), in1=by_rows(odd, 2), op=ALU.max)
            distances(c, gap)
            nc.vector.tensor_tensor(out=u_in[c][:], in0=peak[:], in1=fa_sb[:].unsqueeze(1).to_broadcast([P, PAIRS, PACK]),
                                    op=ALU.mult)

        def quantize_d(c):
            nc.vector.quantize_mx(out=d_codes[c][:].bitcast(FP8X4), scales=d_plane[c][:],
                                  in_=d_in[c][:].rearrange("p b r -> p (b r)"))

        def quantize_u(c):
            cols = slice((c % 2) * PAIRS, (c % 2 + 1) * PAIRS)
            nc.vector.quantize_mx(out=u_codes[c // 2][:, cols].bitcast(FP8X4), scales=u_plane[c // 2][:, cols],
                                  in_=u_in[c][:].rearrange("p b j -> p (b j)"))

        za, ra, zb = {}, {}, {}

        def peak_product(h):
            for g in range(2):
                za[h, g] = ps.tile([P, 2, 2 * PAIRS], F32, name="za%d_%d" % (h, g), tag="za%d" % g)
                for i in (2 * g, 2 * g + 1):
                    nc.tensor.matmul_mx(out=za[h, g][:, i % 2, :], lhsT=wa_codes[:, 2 * P * i : 2 * P * (i + 1)].bitcast(FP4X4),
                                        lhsT_scale=wa_plane[:, 0, P * i : P * (i + 1)], rhs=u_codes[h][:].bitcast(FP8X4),
                                        rhs_scale=u_plane[h][:], start=True, stop=True)

        def relu(h, g):
            ra[h, g] = sb.tile([P, 2, 2 * PAIRS], F32, name="ra%d_%d" % (h, g), align_bytes=64)
            nc.scalar.activation(out=ra[h, g][:], in_=za[h, g][:], func=ACT.Relu)

        def open_bank(h, i, bank):
            zb[h, i] = ps.tile([P, HALF], F32, name="zb%d_%d" % (h, i), tag="zb%d" % bank)

        def second_product(h, i, start=False, stop=False):
            for z in range(PASSES):
                nc.tensor.matmul_mx(out=zb[h, i][:], lhsT=wq_codes[i // 2][:, z, P * (i % 2) : P * (i % 2 + 1)].bitcast(FP8X4),
                                    lhsT_scale=wq_plane[:, z, P * i : P * (i + 1)], rhs=xq_codes[h][:, z, :].bitcast(FP4X4),
                                    rhs_scale=xq_plane[:, z, HALF * h : HALF * (h + 1)],
                                    start=start and z == 0, stop=stop and z == PASSES - 1)

        def distance_product(c, i, start=False, stop=False):
            nc.tensor.matmul_mx(out=zb[c // 2, i][:, (c % 2) * CHUNK : (c % 2 + 1) * CHUNK],
                                lhsT=wb_codes[:, P * i : P * (i + 1)].bitcast(FP8X4), lhsT_scale=wb_plane[:, 0, P * i : P * (i + 1)],
                                rhs=d_codes[c][:].bitcast(FP8X4), rhs_scale=d_plane[c][:], start=start, stop=stop)

        def finish(h, i):
            res = sb.tile([P, 2 * PAIRS, 2], F32, name="res%d_%d" % (h, i), align_bytes=64)
            nc.vector.tensor_tensor(out=res[:], in0=zb[h, i][:].rearrange("p (b e) -> p b e", e=2),
                                    in1=ra[h, i // 2][:, i % 2, :].unsqueeze(2).to_broadcast([P, 2 * PAIRS, 2]), op=ALU.add)
            nc.sync.dma_start(out=out[P * i : P * (i + 1), HALF * h : HALF * (h + 1)], in_=res[:].rearrange("p b e -> p (b e)"))

        prepare(0, (slice(0, 2), slice(2, 4)))
        prepare(1)
        quantize_d(0)
        quantize_u(0)
        for i in range(TILES):
            open_bank(0, i, i)
            distance_product(0, i, start=True)
        prepare(2)
        quantize_d(1)
        quantize_u(1)
        peak_product(0)
        for i in range(TILES):
            distance_product(1, i)
        for i in range(TILES):
            second_product(0, i, stop=True)
        prepare_last(3)
        relu(0, 0)
        interleave_d(3)
        relu(0, 1)
        quantize_u(2)
        quantize_d(2)
        quantize_u(3)
        peak_product(1)
        relu(1, 0)
        relu(1, 1)
        for i in range(2):
            open_bank(1, i, TILES + i)
            second_product(1, i, start=True)
            distance_product(2, i)
        finish(0, 0)
        quantize_d(3)
        finish(0, 1)
        for i in range(2):
            distance_product(3, i, stop=True)
        for i in range(2, TILES):
            open_bank(1, i, i - 2)
            second_product(1, i, start=True)
            distance_product(2, i)
            distance_product(3, i, stop=True)
        finish(0, 2)
        finish(0, 3)
        for i in range(TILES):
            finish(1, i)
